import numpy as np
import ml_dtypes


def mxq(x, axis, fmt="e4m3"):
    dtype, down = {"e4m3": (ml_dtypes.float8_e4m3fn, 7), "e5m2": (ml_dtypes.float8_e5m2, 14)}[fmt]
    v = np.moveaxis(np.asarray(x, np.float32).astype(ml_dtypes.bfloat16).astype(np.float64), axis, -1)
    blocks = v.reshape(v.shape[:-1] + (-1, 32))
    amax = np.abs(blocks).max(-1, keepdims=True)
    byte = np.maximum(np.where(amax > 0, np.frexp(amax)[1] - 1 + 127, 0) - down, 1)
    scale = np.exp2(byte - 127.0)
    codes = (blocks / scale).astype(np.float32).astype(dtype).astype(np.float64)
    return np.moveaxis((codes * scale).reshape(v.shape), -1, axis)


WIDE = False


def mx_kscale(k):
    if not WIDE:
        return np.ones(k)
    levels = np.array([10, -10, 5, -5, 0])
    if k % 512:
        return np.exp2(np.random.permutation(np.resize(levels, k // 32))).repeat(32)
    a = np.empty((k // 512, 16))
    for p in range(k // 512):
        a[p, :8] = np.random.permutation(np.resize(levels, 8))
        for g in range(8):
            far = levels[np.abs(levels - a[p, g]) >= 10]
            a[p, g + 8] = far[np.random.randint(len(far))]
    return np.exp2(a.ravel()).repeat(32)


def f64(x):
    return np.asarray(x).astype(np.float64)


def striped8(idx):
    return np.asarray(idx).reshape(8, -1, 16).transpose(0, 2, 1).reshape(128, -1).astype(np.uint16)


def unstriped8(offs):
    return offs.reshape(8, 16, -1).transpose(0, 2, 1).reshape(8, -1).astype(np.int64)


def pick8(x, idx, run):
    r = np.arange(len(x))
    return x[r[:, None], idx[r % (8 * run) // run]]


E2M1 = np.array([0.0, 0.5, 1.0, 1.5, 2.0, 3.0, 4.0, 6.0, -0.0, -0.5, -1.0, -1.5, -2.0, -3.0, -4.0, -6.0])


def pack_weight(w, fmt):
    k, n = w.shape
    w = f64(np.asarray(w, np.float32).astype(ml_dtypes.bfloat16)).reshape(k // 32, 32, n)
    amax = np.abs(w).max(1)
    if fmt == "e4m3":
        byte = np.frexp(amax)[1] - 1 + 127 - 7
    else:
        mant, ex = np.frexp(amax / 6.0)
        byte = np.where(mant > 0.5, ex, ex - 1) + 127
    byte = np.clip(np.where(amax > 0, byte, 1), 1, 254)
    scaled = (w * np.exp2(127.0 - byte)[:, None, :]).reshape(k, n).astype(np.float32)
    by_word = np.ascontiguousarray(scaled.reshape(k // 512, 128, 4, n).transpose(0, 1, 3, 2))
    if fmt == "e4m3":
        words = by_word.astype(ml_dtypes.float8_e4m3fn).view(np.uint8)
    else:
        c = by_word.astype(ml_dtypes.float4_e2m1fn).view(np.uint8) & 0xF
        words = (c[..., 0::2] | (c[..., 1::2] << 4)).reshape(k // 512, 128, 2 * n)
    return np.ascontiguousarray(words), np.ascontiguousarray(byte.astype(np.uint8).reshape(k // 512, 16, n))


def unpack_weight(words, scales, fmt):
    g, _, n = scales.shape
    words = np.ascontiguousarray(words).reshape(g, 128, n, -1)
    if fmt == "e4m3":
        vals = words.view(ml_dtypes.float8_e4m3fn).astype(np.float64)
    else:
        nib = np.empty((g, 128, n, 4), np.uint8)
        nib[..., 0::2] = words & 0xF
        nib[..., 1::2] = words >> 4
        vals = E2M1[nib]
    vals = vals * np.repeat(np.exp2(scales.astype(np.float64) - 127.0), 8, axis=1)[..., None]
    return vals.transpose(0, 1, 3, 2).reshape(g * 512, n)


def sigmoid(v):
    return 1.0 / (1.0 + np.exp(-v))


D, V, Q, I = 512, 2048, 128, 512


def setup_inputs():
    n = np.random.standard_normal
    idx = np.stack([np.random.permutation(V)[:I] for _ in range(8)])
    idx2 = np.stack([np.random.permutation(V)[:I] for _ in range(8)])
    fd = mx_kscale(D)
    vocp = pack_weight(n((D, V)) / fd[:, None], "e4m3")
    return {
        "hid": (n((D, Q)) * 1.0 / np.sqrt(D) * fd[:, None]).astype(np.float32),
        "voc_words": vocp[0],
        "voc_scales": vocp[1],
        "sw": (np.random.uniform(0.5, 2.0, (1, I))).astype(np.float32),
        "dhid": (n((D, Q)) * 1.0 / np.sqrt(D) * fd[:, None]).astype(np.float32),
        "base": (0.5 * n((Q, V))).astype(np.float32),
        "offs": striped8(idx),
        "offs2": striped8(idx2),
    }


def reference(hid, voc_words, voc_scales, sw, dhid, base, offs, offs2):
    idx = unstriped8(offs)
    idx2 = unstriped8(offs2)
    vocu = unpack_weight(voc_words, voc_scales, "e4m3")
    hidq = mxq(f64(hid), 0, "e4m3")
    a = hidq.T @ vocu
    dhidq = mxq(f64(dhid), 0, "e4m3")
    ta = dhidq.T @ vocu
    m1 = np.max(a, axis=1, keepdims=True)
    p = np.exp(a - m1)
    z = np.sum(p, axis=1, keepdims=True)
    px = np.exp(pick8(a, idx, 16) - m1)
    px2 = np.exp(pick8(a, idx2, 16) - m1)
    u1 = sigmoid((px2 - px) / z * 512.0)
    dpx2 = f64(sw) * u1 * (1.0 - u1) * 512.0 / z
    dpx = f64(sw) * u1 * (1.0 - u1) * 512.0 / z * (-1.0)
    dz = np.sum(f64(sw) * u1 * (1.0 - u1) * 512.0 * (px2 - px) / np.square(z) * (-1.0), axis=1, keepdims=True)
    xp = ta * p
    xz = np.sum(xp, axis=1, keepdims=True)
    xpx = pick8(ta, idx, 16) * px
    xpx2 = pick8(ta, idx2, 16) * px2
    xu1 = (xpx2 - xpx - xz * (px2 - px) / z) / z * 512.0 * u1 * (1.0 - u1)
    xdpx2 = ((xu1 * f64(sw) * (1.0 - u1) + xu1 * (-1.0) * f64(sw) * u1) * 512.0 - xz * f64(sw) * u1 * (1.0 - u1) * 512.0 / z) / z
    xdpx = ((xu1 * f64(sw) * (1.0 - u1) + xu1 * (-1.0) * f64(sw) * u1) * 512.0 - xz * f64(sw) * u1 * (1.0 - u1) * 512.0 / z) / z * (-1.0)
    xdz = np.sum(((xu1 * f64(sw) * (1.0 - u1) + xu1 * (-1.0) * f64(sw) * u1) * 512.0 * (px2 - px) + (xpx2 - xpx) * f64(sw) * u1 * (1.0 - u1) * 512.0 - xz * z * 2.0 * f64(sw) * u1 * (1.0 - u1) * 512.0 * (px2 - px) / np.square(z)) / np.square(z) * (-1.0), axis=1, keepdims=True)
    xe1 = xdpx2 * px2 + xpx2 * dpx2
    xs1 = np.zeros((Q, V))
    xs1[np.arange(Q)[:, None], idx2[np.arange(Q) % 128 // 16]] = xe1
    xe2 = xdpx * px + xpx * dpx
    xs2 = np.zeros((Q, V))
    xs2[np.arange(Q)[:, None], idx[np.arange(Q) % 128 // 16]] = xe2
    xda = xdz * p + xp * dz + xs1 + xs2
    y = xda * 2.0 + f64(base)
    return y

@@ -1,0 +1,245 @@
+from contextlib import ExitStack
+
+import concourse.mybir as mybir
+from concourse.masks import make_identity
+
+D, V, Q, I = 512, 2048, 128, 512
+FLOPS = 2 * 2 * D * Q * V
+
+F32 = mybir.dt.float32
+BF16 = mybir.dt.bfloat16
+I32 = mybir.dt.int32
+U32 = mybir.dt.uint32
+U16 = mybir.dt.uint16
+U8 = mybir.dt.uint8
+FP8X4 = mybir.dt.float8_e4m3fn_x4
+ACT = mybir.ActivationFunctionType
+ALU = mybir.AluOpType
+AX = mybir.AxisListType
+
+P = 128
+PACK = 4
+BANK = 512
+CHUNKS = V // BANK
+BLOCKS = BANK // P
+
+
+def tile_attend_hvrankshares_heads_kernel(tc, hid, voc_words, voc_scales, sw, dhid, base, offs, offs2, out):
+    nc = tc.nc
+    with ExitStack() as ctx:
+        sb = ctx.enter_context(tc.tile_pool(name="sb", bufs=1))
+        ps = ctx.enter_context(tc.psum_pool(name="ps", bufs=1))
+
+        def cols(c):
+            return slice(c * BANK, (c + 1) * BANK)
+
+        def blk(j):
+            return slice(j * P, (j + 1) * P)
+
+        planes = sb.tile([P, BANK], U8, name="planes", align_bytes=64)
+        nc.gpsimd.memset(planes[:].bitcast(I32), 0)
+        hid_raw = sb.tile([P, PACK, Q], F32, name="hid_raw")
+        dhid_raw = sb.tile([P, PACK, Q], F32, name="dhid_raw")
+        words = [sb.tile([P, BANK], U32, name="words%d" % c, align_bytes=64) for c in range(CHUNKS)]
+        voc32 = voc_words[0].rearrange("p n t -> p (n t)").bitcast(I32)
+        scales32 = voc_scales[0].bitcast(I32)
+
+        nc.sync.dma_start(out=hid_raw[:], in_=hid.rearrange("(p j) q -> p j q", j=PACK))
+        for quad in range(4):
+            nc.scalar.dma_start(
+                out=planes[32 * quad : 32 * quad + 16, :].bitcast(I32),
+                in_=scales32[4 * quad : 4 * quad + 4, :].rearrange("r (c n) -> c r n", c=CHUNKS),
+            )
+        for c in range(CHUNKS):
+            if c == CHUNKS - 1:
+                nc.sync.dma_start(out=dhid_raw[:], in_=dhid.rearrange("(p j) q -> p j q", j=PACK))
+            nc.sync.dma_start(out=words[c][:].bitcast(I32), in_=voc32[:, cols(c)])
+        list1 = sb.tile([P, I // 16], U16, name="list1")
+        list2 = sb.tile([P, I // 16], U16, name="list2")
+        nc.sync.dma_start(list1[:], offs)
+        nc.sync.dma_start(list2[:], offs2)
+        w_cols = sb.tile([P, 4], F32, name="w_cols")
+        nc.sync.dma_start(out=w_cols[:], in_=sw.rearrange("o (p c) -> (o p) c", c=4))
+        base_sb = [sb.tile([P, BANK], F32, name="base%d" % c) for c in range(CHUNKS)]
+        for c in range(CHUNKS):
+            nc.sync.dma_start(out=base_sb[c][:], in_=base[:, cols(c)])
+
+        factors = sb.tile([P, 3], F32, name="factors")
+        for j, value in enumerate((256.0, -256.0, -1.0)):
+            nc.gpsimd.memset(factors[:, j : j + 1], value)
+        warm = sb.tile([P, 1], F32, name="warm")
+        nc.scalar.activation(out=warm[:], in_=factors[:, 2:3], func=ACT.Exp)
+
+        def quantise(raw, cast, tag):
+            grouped = sb.tile([P, Q, PACK], BF16, name=tag + "_bf", tag=tag + "_bf", align_bytes=64)
+            cast(out=grouped[:], in_=raw[:].rearrange("p j q -> p q j"))
+            codes = sb.tile([P, Q], U32, name=tag + "_codes", align_bytes=64)
+            scales = sb.tile([P, Q], U8, name=tag + "_scales", tag=tag + "_scales", align_bytes=64)
+            nc.vector.quantize_mx(
+                out=codes[:].bitcast(FP8X4), scales=scales[:], in_=grouped[:].rearrange("p q j -> p (q j)")
+            )
+            return codes, scales
+
+        def score(operand, c, tag):
+            codes, scales = operand
+            bank = ps.tile([P, BANK], F32, name=tag, tag=tag)
+            nc.tensor.matmul_mx(
+                out=bank[:],
+                lhsT=codes[:].bitcast(FP8X4),
+                lhsT_scale=scales[:],
+                rhs=words[c][:].bitcast(FP8X4),
+                rhs_scale=planes[4 * c : P, :],
+                start=True,
+                stop=True,
+            )
+            return bank
+
+        hq = quantise(hid_raw, nc.vector.tensor_copy, "hid")
+        ident = sb.tile([P, P], F32, name="ident", tag="hid_bf", align_bytes=64)
+        make_identity(nc, ident[:])
+        a = sb.tile([P, V], F32, name="a")
+        ta = sb.tile([P, V], F32, name="ta")
+        maxes = sb.tile([P, CHUNKS], F32, name="maxes")
+        dq = None
+        for c in range(CHUNKS):
+            if c == CHUNKS - 1:
+                dq = quantise(dhid_raw, nc.scalar.copy, "dhid")
+            bank = score(hq, c, "lo%d" % c)
+            nc.vector.tensor_scalar(
+                out=a[:, cols(c)], in0=bank[:], scalar1=1.0, scalar2=None, op0=ALU.mult, op1=ALU.max,
+                accum_out=maxes[:, c : c + 1],
+            )
+        neg_max = sb.tile([P, 1], F32, name="neg_max")
+        nc.vector.tensor_reduce(out=neg_max[:], in_=maxes[:], axis=AX.X, op=ALU.max, negate=True)
+        for c in range(CHUNKS):
+            bank = score(dq, c, "hi%d" % c)
+            nc.scalar.copy(out=ta[:, cols(c)], in_=bank[:])
+        placed1 = sb.tile([P, V], F32, name="placed1", tag="dhid_bf", align_bytes=64)
+        placed2 = sb.tile([P, V], F32, name="placed2", tag="dhid_scales", align_bytes=64)
+        nc.gpsimd.memset(placed1[:], 0.0)
+        nc.gpsimd.memset(placed2[:], 0.0)
+        ax = sb.tile([P, 2, I], F32, name="ax")
+        nc.vector.tensor_copy(out=ax[:, 0, :], in_=a[:].indirect(list1[:]))
+        nc.vector.tensor_copy(out=ax[:, 1, :], in_=a[:].indirect(list2[:]))
+
+        p = sb.tile([P, V], F32, name="p")
+        z = sb.tile([P, 1], F32, name="z")
+        nc.scalar.activation(out=p[:], in_=a[:], func=ACT.Exp, bias=neg_max[:], accum_out=z[:])
+        px = sb.tile([P, 2, I], F32, name="px")
+        nc.scalar.activation(out=px[:], in_=ax[:], func=ACT.Exp, bias=neg_max[:])
+        px1, px2 = px[:, 0, :], px[:, 1, :]
+        tx = sb.tile([P, 2, I], F32, name="tx")
+        nc.vector.tensor_copy(out=tx[:, 0, :], in_=ta[:].indirect(list1[:]))
+        nc.vector.tensor_copy(out=tx[:, 1, :], in_=ta[:].indirect(list2[:]))
+        r = sb.tile([P, 1], F32, name="r")
+        nc.vector.reciprocal(out=r[:], in_=z[:])
+        rs = sb.tile([P, 3], F32, name="rs")
+        nc.scalar.activation(out=rs[:], in_=factors[:], func=ACT.Copy, scale=r[:])
+        rho, neg_rho, neg_r = rs[:, 0:1], rs[:, 1:2], rs[:, 2:3]
+
+        w_bank = ps.tile([P, 4, P], F32, name="w_bank", tag="hi0")
+        for c in range(4):
+            nc.tensor.transpose(w_bank[:, c, :], w_cols[:, c : c + 1].to_broadcast([P, P]), ident[:])
+
+        sums = [ps.tile([P, BLOCKS, P], F32, name="sum%d" % c, tag="lo%d" % c) for c in range(CHUNKS)]
+
+        def add_turned(c, j, block, start=False, stop=False):
+            nc.tensor.matmul(sums[c][:, j, :], block, ident[:], start=start, stop=stop, is_transpose=True)
+
+        for c in range(CHUNKS):
+            for j in range(BLOCKS):
+                add_turned(c, j, base_sb[c][:, blk(j)], start=(j == 0))
+
+        xp = [sb.tile([P, BANK], F32, name="xp%d" % c) for c in range(CHUNKS)]
+        xz = sb.tile([P, CHUNKS], F32, name="xz")
+
+        def make_xp(c):
+            nc.vector.scalar_tensor_tensor(
+                out=xp[c][:], in0=ta[:, cols(c)], scalar=1.0, in1=p[:, cols(c)], op0=ALU.mult, op1=ALU.mult,
+                accum_out=xz[:, c : c + 1],
+            )
+
+        make_xp(0)
+        dp = sb.tile([P, I], F32, name="dp")
+        nc.vector.tensor_tensor(out=dp[:], in0=px2, in1=px1, op=ALU.subtract)
+        for c in range(1, CHUNKS):
+            make_xp(c)
+        th = sb.tile([P, I], F32, name="th")
+        th2 = sb.tile([P, I], F32, name="th2")
+        nc.scalar.activation(out=th[:], in_=dp[:], func=ACT.Tanh, scale=rho)
+        nc.scalar.activation(out=th2[:], in_=th[:], func=ACT.Square)
+        junk4 = sb.tile([P, 4], F32, name="junk4")
+        neg_mu = sb.tile([P, 1], F32, name="neg_mu")
+        nc.scalar.activation(out=junk4[:], in_=xz[:], func=ACT.Copy, scale=neg_r, accum_out=neg_mu[:])
+
+        g = sb.tile([P, I], F32, name="g")
+        nc.vector.scalar_tensor_tensor(
+            out=g[:].rearrange("p (n c) -> p n c", c=4),
+            in0=th2[:].rearrange("p (n c) -> p n c", c=4),
+            scalar=-1.0,
+            in1=w_bank[:].rearrange("p c n -> p n c"),
+            op0=ALU.add,
+            op1=ALU.mult,
+        )
+        gp = sb.tile([P, 2, I], F32, name="gp")
+        b_parts = sb.tile([P, 2], F32, name="b_parts")
+        for k, (pxk, factor) in enumerate(((px1, rho), (px2, neg_rho))):
+            nc.vector.scalar_tensor_tensor(
+                out=gp[:, k, :], in0=g[:], scalar=factor, in1=pxk, op0=ALU.mult, op1=ALU.mult,
+                accum_out=b_parts[:, k : k + 1],
+            )
+        s_parts = sb.tile([P, 5], F32, name="s_parts")
+        y = sb.tile([P, 2, I], F32, name="y")
+        for k in range(2):
+            nc.vector.scalar_tensor_tensor(
+                out=y[:, k, :], in0=tx[:, k, :], scalar=neg_mu[:], in1=gp[:, k, :], op0=ALU.add, op1=ALU.mult,
+                accum_out=s_parts[:, k : k + 1],
+            )
+        junk2 = sb.tile([P, 2], F32, name="junk2")
+        b_sum = sb.tile([P, 1], F32, name="b_sum")
+        beta = sb.tile([P, 1], F32, name="beta")
+        nc.scalar.activation(out=junk2[:], in_=b_parts[:], func=ACT.Copy, accum_out=b_sum[:])
+        nc.scalar.activation(out=beta[:], in_=b_sum[:], func=ACT.Copy, scale=neg_r)
+        nc.scalar.activation(out=s_parts[:, 4:5], in_=b_sum[:], func=ACT.Copy, scale=neg_mu[:])
+        for c in range(CHUNKS):
+            scaled = sb.tile([P, BANK], F32, name="bxp%d" % c)
+            nc.scalar.activation(out=scaled[:], in_=xp[c][:], func=ACT.Copy, scale=beta[:])
+            for j in range(BLOCKS):
+                add_turned(c, j, scaled[:, blk(j)])
+
+        eg = sb.tile([P, I], F32, name="eg")
+        nc.vector.tensor_tensor(out=eg[:], in0=y[:, 0, :], in1=y[:, 1, :], op=ALU.add)
+        kk = sb.tile([P, I], F32, name="kk")
+        nc.vector.scalar_tensor_tensor(out=kk[:], in0=th[:], scalar=rho, in1=eg[:], op0=ALU.mult, op1=ALU.mult)
+        m = sb.tile([P, 2, I], F32, name="m")
+        for k, (pxk, factor) in enumerate(((px1, 2.0), (px2, -2.0))):
+            nc.vector.scalar_tensor_tensor(
+                out=m[:, k, :], in0=kk[:], scalar=factor, in1=pxk, op0=ALU.mult, op1=ALU.mult,
+                accum_out=s_parts[:, 2 + k : 3 + k],
+            )
+        nc.vector.tensor_tensor(out=placed1[:].indirect(list1[:]), in0=y[:, 0, :], in1=m[:, 0, :], op=ALU.add)
+        nc.vector.tensor_tensor(out=placed2[:].indirect(list2[:]), in0=y[:, 1, :], in1=m[:, 1, :], op=ALU.add)
+
+        junk5 = sb.tile([P, 5], F32, name="junk5")
+        alpha = sb.tile([P, 1], F32, name="alpha")
+        nc.scalar.activation(out=junk5[:], in_=s_parts[:], func=ACT.Copy, scale=neg_r, accum_out=alpha[:])
+        p_blocks = p[:].rearrange("p (c j n) -> p c j n", c=CHUNKS, j=BLOCKS)
+        for j in range(BLOCKS):
+            scaled = sb.tile([P, CHUNKS, P], F32, name="ap%d" % j)
+            nc.scalar.activation(out=scaled[:], in_=p_blocks[:, :, j, :], func=ACT.Copy, scale=alpha[:])
+            for c in range(CHUNKS):
+                add_turned(c, j, scaled[:, c, :])
+        for c in range(CHUNKS):
+            for j in range(BLOCKS):
+                add_turned(c, j, placed1[:, c * BANK + j * P : c * BANK + (j + 1) * P], stop=(j == BLOCKS - 1))
+        for c in range(CHUNKS):
+            turned = sb.tile([P, BLOCKS, P], F32, name="turned%d" % c)
+            nc.scalar.copy(out=turned[:], in_=sums[c][:])
+            back = ps.tile([P, BLOCKS, P], F32, name="back%d" % c, tag="hi%d" % c)
+            for j in range(BLOCKS):
+                nc.tensor.transpose(back[:, j, :], turned[:, j, :], ident[:])
+            result = sb.tile([P, BANK], F32, name="result%d" % c)
+            nc.vector.tensor_tensor(
+                out=result[:], in0=back[:].rearrange("p j n -> p (j n)"), in1=placed2[:, cols(c)], op=ALU.add
+            )
+            nc.sync.dma_start(out=out[:, cols(c)], in_=result[:])

@@ -40,13 +40,13 @@ def tile_attend_hvrankshares_heads_kernel(tc, hid, voc_words, voc_scales, sw, dh
         nc.gpsimd.memset(planes[:].bitcast(I32), 0)
         hid_raw = sb.tile([P, PACK, Q], F32, name="hid_raw")
         dhid_raw = sb.tile([P, PACK, Q], F32, name="dhid_raw")
-        words = [sb.tile([P, BANK], U32, name="words%d" % c, align_bytes=64) for c in range(CHUNKS)]
+        words = [sb.tile([P, BANK], U32, name="words%d" % c, tag="words%d" % c, align_bytes=64) for c in range(CHUNKS)]
         voc32 = voc_words[0].rearrange("p n t -> p (n t)").bitcast(I32)
         scales32 = voc_scales[0].bitcast(I32)
 
         nc.sync.dma_start(out=hid_raw[:], in_=hid.rearrange("(p j) q -> p j q", j=PACK))
         for quad in range(4):
-            nc.scalar.dma_start(
+            nc.sync.dma_start(
                 out=planes[32 * quad : 32 * quad + 16, :].bitcast(I32),
                 in_=scales32[4 * quad : 4 * quad + 4, :].rearrange("r (c n) -> c r n", c=CHUNKS),
             )
@@ -60,12 +60,11 @@ def tile_attend_hvrankshares_heads_kernel(tc, hid, voc_words, voc_scales, sw, dh
         nc.sync.dma_start(list2[:], offs2)
         w_cols = sb.tile([P, 4], F32, name="w_cols")
         nc.sync.dma_start(out=w_cols[:], in_=sw.rearrange("o (p c) -> (o p) c", c=4))
-        base_sb = [sb.tile([P, BANK], F32, name="base%d" % c) for c in range(CHUNKS)]
-        for c in range(CHUNKS):
-            nc.sync.dma_start(out=base_sb[c][:], in_=base[:, cols(c)])
+        base_sb = sb.tile([P, V], F32, name="base_sb")
+        nc.sync.dma_start(out=base_sb[:], in_=base)
 
-        factors = sb.tile([P, 3], F32, name="factors")
-        for j, value in enumerate((256.0, -256.0, -1.0)):
+        factors = sb.tile([P, 5], F32, name="factors")
+        for j, value in enumerate((256.0, -256.0, -1.0, 512.0, -512.0)):
             nc.gpsimd.memset(factors[:, j : j + 1], value)
         warm = sb.tile([P, 1], F32, name="warm")
         nc.scalar.activation(out=warm[:], in_=factors[:, 2:3], func=ACT.Exp)
@@ -73,7 +72,7 @@ def tile_attend_hvrankshares_heads_kernel(tc, hid, voc_words, voc_scales, sw, dh
         def quantise(raw, cast, tag):
             grouped = sb.tile([P, Q, PACK], BF16, name=tag + "_bf", tag=tag + "_bf", align_bytes=64)
             cast(out=grouped[:], in_=raw[:].rearrange("p j q -> p q j"))
-            codes = sb.tile([P, Q], U32, name=tag + "_codes", align_bytes=64)
+            codes = sb.tile([P, Q], U32, name=tag + "_codes", tag="codes", align_bytes=64)
             scales = sb.tile([P, Q], U8, name=tag + "_scales", tag=tag + "_scales", align_bytes=64)
             nc.vector.quantize_mx(
                 out=codes[:].bitcast(FP8X4), scales=scales[:], in_=grouped[:].rearrange("p q j -> p (q j)")
@@ -95,34 +94,34 @@ def tile_attend_hvrankshares_heads_kernel(tc, hid, voc_words, voc_scales, sw, dh
             return bank
 
         hq = quantise(hid_raw, nc.vector.tensor_copy, "hid")
-        ident = sb.tile([P, P], F32, name="ident", tag="hid_bf", align_bytes=64)
-        make_identity(nc, ident[:])
         a = sb.tile([P, V], F32, name="a")
         ta = sb.tile([P, V], F32, name="ta")
         maxes = sb.tile([P, CHUNKS], F32, name="maxes")
         dq = None
         for c in range(CHUNKS):
+            bank = score(hq, c, "bank%d" % c)
             if c == CHUNKS - 1:
                 dq = quantise(dhid_raw, nc.scalar.copy, "dhid")
-            bank = score(hq, c, "lo%d" % c)
             nc.vector.tensor_scalar(
                 out=a[:, cols(c)], in0=bank[:], scalar1=1.0, scalar2=None, op0=ALU.mult, op1=ALU.max,
                 accum_out=maxes[:, c : c + 1],
             )
-        neg_max = sb.tile([P, 1], F32, name="neg_max")
-        nc.vector.tensor_reduce(out=neg_max[:], in_=maxes[:], axis=AX.X, op=ALU.max, negate=True)
+        ta_banks = [score(dq, c, "bank%d" % (CHUNKS + c)) for c in range(CHUNKS)]
         for c in range(CHUNKS):
-            bank = score(dq, c, "hi%d" % c)
-            nc.scalar.copy(out=ta[:, cols(c)], in_=bank[:])
+            nc.scalar.copy(out=ta[:, cols(c)], in_=ta_banks[c][:])
         placed1 = sb.tile([P, V], F32, name="placed1", tag="dhid_bf", align_bytes=64)
-        placed2 = sb.tile([P, V], F32, name="placed2", tag="dhid_scales", align_bytes=64)
+        placed2 = sb.tile([P, V], F32, name="placed2", tag="words3", align_bytes=64)
         nc.gpsimd.memset(placed1[:], 0.0)
+        ident = sb.tile([P, P], F32, name="ident", tag="dhid_scales", align_bytes=64)
+        make_identity(nc, ident[:])
         nc.gpsimd.memset(placed2[:], 0.0)
         ax = sb.tile([P, 2, I], F32, name="ax")
         nc.vector.tensor_copy(out=ax[:, 0, :], in_=a[:].indirect(list1[:]))
+        neg_max = sb.tile([P, 1], F32, name="neg_max")
+        nc.vector.tensor_reduce(out=neg_max[:], in_=maxes[:], axis=AX.X, op=ALU.max, negate=True)
         nc.vector.tensor_copy(out=ax[:, 1, :], in_=a[:].indirect(list2[:]))
 
-        p = sb.tile([P, V], F32, name="p")
+        p = sb.tile([P, V], F32, name="p", tag="codes", align_bytes=64)
         z = sb.tile([P, 1], F32, name="z")
         nc.scalar.activation(out=p[:], in_=a[:], func=ACT.Exp, bias=neg_max[:], accum_out=z[:])
         px = sb.tile([P, 2, I], F32, name="px")
@@ -133,29 +132,29 @@ def tile_attend_hvrankshares_heads_kernel(tc, hid, voc_words, voc_scales, sw, dh
         nc.vector.tensor_copy(out=tx[:, 1, :], in_=ta[:].indirect(list2[:]))
         r = sb.tile([P, 1], F32, name="r")
         nc.vector.reciprocal(out=r[:], in_=z[:])
-        rs = sb.tile([P, 3], F32, name="rs")
+        rs = sb.tile([P, 5], F32, name="rs")
         nc.scalar.activation(out=rs[:], in_=factors[:], func=ACT.Copy, scale=r[:])
         rho, neg_rho, neg_r = rs[:, 0:1], rs[:, 1:2], rs[:, 2:3]
 
-        w_bank = ps.tile([P, 4, P], F32, name="w_bank", tag="hi0")
+        w_bank = ps.tile([P, 4, P], F32, name="w_bank", tag="bank0")
         for c in range(4):
             nc.tensor.transpose(w_bank[:, c, :], w_cols[:, c : c + 1].to_broadcast([P, P]), ident[:])
 
-        sums = [ps.tile([P, BLOCKS, P], F32, name="sum%d" % c, tag="lo%d" % c) for c in range(CHUNKS)]
+        sums = [ps.tile([P, BLOCKS, P], F32, name="sum%d" % c, tag="bank%d" % b) for c, b in enumerate((1, 2, 3, 4))]
 
         def add_turned(c, j, block, start=False, stop=False):
             nc.tensor.matmul(sums[c][:, j, :], block, ident[:], start=start, stop=stop, is_transpose=True)
 
         for c in range(CHUNKS):
             for j in range(BLOCKS):
-                add_turned(c, j, base_sb[c][:, blk(j)], start=(j == 0))
+                add_turned(c, j, base_sb[:, c * BANK + j * P : c * BANK + (j + 1) * P], start=(j == 0))
 
         xp = [sb.tile([P, BANK], F32, name="xp%d" % c) for c in range(CHUNKS)]
         xz = sb.tile([P, CHUNKS], F32, name="xz")
 
         def make_xp(c):
             nc.vector.scalar_tensor_tensor(
-                out=xp[c][:], in0=ta[:, cols(c)], scalar=1.0, in1=p[:, cols(c)], op0=ALU.mult, op1=ALU.mult,
+                out=xp[c][:], in0=ta_banks[c][:], scalar=1.0, in1=p[:, cols(c)], op0=ALU.mult, op1=ALU.mult,
                 accum_out=xz[:, c : c + 1],
             )
 
@@ -168,6 +167,9 @@ def tile_attend_hvrankshares_heads_kernel(tc, hid, voc_words, voc_scales, sw, dh
         th2 = sb.tile([P, I], F32, name="th2")
         nc.scalar.activation(out=th[:], in_=dp[:], func=ACT.Tanh, scale=rho)
         nc.scalar.activation(out=th2[:], in_=th[:], func=ACT.Square)
+        tp = sb.tile([P, 2, I], F32, name="tp")
+        for k in range(2):
+            nc.gpsimd.tensor_tensor(out=tp[:, k, :], in0=th[:], in1=px[:, k, :], op=ALU.mult)
         junk4 = sb.tile([P, 4], F32, name="junk4")
         neg_mu = sb.tile([P, 1], F32, name="neg_mu")
         nc.scalar.activation(out=junk4[:], in_=xz[:], func=ACT.Copy, scale=neg_r, accum_out=neg_mu[:])
@@ -190,10 +192,11 @@ def tile_attend_hvrankshares_heads_kernel(tc, hid, voc_words, voc_scales, sw, dh
             )
         s_parts = sb.tile([P, 5], F32, name="s_parts")
         y = sb.tile([P, 2, I], F32, name="y")
-        for k in range(2):
+        halves = [slice(h * I // 2, (h + 1) * I // 2) for h in range(2)]
+        for h, half in enumerate(halves):
             nc.vector.scalar_tensor_tensor(
-                out=y[:, k, :], in0=tx[:, k, :], scalar=neg_mu[:], in1=gp[:, k, :], op0=ALU.add, op1=ALU.mult,
-                accum_out=s_parts[:, k : k + 1],
+                out=y[:, :, half], in0=tx[:, :, half], scalar=neg_mu[:], in1=gp[:, :, half],
+                op0=ALU.add, op1=ALU.mult, accum_out=s_parts[:, h : h + 1],
             )
         junk2 = sb.tile([P, 2], F32, name="junk2")
         b_sum = sb.tile([P, 1], F32, name="b_sum")
@@ -208,13 +211,12 @@ def tile_attend_hvrankshares_heads_kernel(tc, hid, voc_words, voc_scales, sw, dh
                 add_turned(c, j, scaled[:, blk(j)])
 
         eg = sb.tile([P, I], F32, name="eg")
-        nc.vector.tensor_tensor(out=eg[:], in0=y[:, 0, :], in1=y[:, 1, :], op=ALU.add)
-        kk = sb.tile([P, I], F32, name="kk")
-        nc.vector.scalar_tensor_tensor(out=kk[:], in0=th[:], scalar=rho, in1=eg[:], op0=ALU.mult, op1=ALU.mult)
+        for half in halves:
+            nc.vector.tensor_tensor(out=eg[:, half], in0=y[:, 0, half], in1=y[:, 1, half], op=ALU.add)
         m = sb.tile([P, 2, I], F32, name="m")
-        for k, (pxk, factor) in enumerate(((px1, 2.0), (px2, -2.0))):
+        for k in range(2):
             nc.vector.scalar_tensor_tensor(
-                out=m[:, k, :], in0=kk[:], scalar=factor, in1=pxk, op0=ALU.mult, op1=ALU.mult,
+                out=m[:, k, :], in0=tp[:, k, :], scalar=rs[:, 3 + k : 4 + k], in1=eg[:], op0=ALU.mult, op1=ALU.mult,
                 accum_out=s_parts[:, 2 + k : 3 + k],
             )
         nc.vector.tensor_tensor(out=placed1[:].indirect(list1[:]), in0=y[:, 0, :], in1=m[:, 0, :], op=ALU.add)
@@ -235,11 +237,18 @@ def tile_attend_hvrankshares_heads_kernel(tc, hid, voc_words, voc_scales, sw, dh
         for c in range(CHUNKS):
             turned = sb.tile([P, BLOCKS, P], F32, name="turned%d" % c)
             nc.scalar.copy(out=turned[:], in_=sums[c][:])
-            back = ps.tile([P, BLOCKS, P], F32, name="back%d" % c, tag="hi%d" % c)
+            back = ps.tile([P, BLOCKS, P], F32, name="back%d" % c, tag="bank%d" % (5, 6, 7, 0)[c])
             for j in range(BLOCKS):
                 nc.tensor.transpose(back[:, j, :], turned[:, j, :], ident[:])
-            result = sb.tile([P, BANK], F32, name="result%d" % c)
-            nc.vector.tensor_tensor(
-                out=result[:], in0=back[:].rearrange("p j n -> p (j n)"), in1=placed2[:, cols(c)], op=ALU.add
-            )
-            nc.sync.dma_start(out=out[:, cols(c)], in_=result[:])
+            pieces = 2 if c in (0, CHUNKS - 1) else 1
+            width = BANK // pieces
+            for h in range(pieces):
+                result = sb.tile([P, width], F32, name="result%d_%d" % (c, h))
+                where = slice(c * BANK + h * width, c * BANK + (h + 1) * width)
+                nc.vector.tensor_tensor(
+                    out=result[:],
+                    in0=back[:].rearrange("p j n -> p (j n)")[:, h * width : (h + 1) * width],
+                    in1=placed2[:, where],
+                    op=ALU.add,
+                )
+                nc.sync.dma_start(out=out[:, where], in_=result[:])

@@ -51,7 +51,7 @@ def tile_attend_hvrankshares_heads_kernel(tc, hid, voc_words, voc_scales, sw, dh
                 in_=scales32[4 * quad : 4 * quad + 4, :].rearrange("r (c n) -> c r n", c=CHUNKS),
             )
         for c in range(CHUNKS):
-            if c == CHUNKS - 1:
+            if c == 2:
                 nc.sync.dma_start(out=dhid_raw[:], in_=dhid.rearrange("(p j) q -> p j q", j=PACK))
             nc.sync.dma_start(out=words[c][:].bitcast(I32), in_=voc32[:, cols(c)])
         list1 = sb.tile([P, I // 16], U16, name="list1")
@@ -60,11 +60,9 @@ def tile_attend_hvrankshares_heads_kernel(tc, hid, voc_words, voc_scales, sw, dh
         nc.sync.dma_start(list2[:], offs2)
         w_cols = sb.tile([P, 4], F32, name="w_cols")
         nc.sync.dma_start(out=w_cols[:], in_=sw.rearrange("o (p c) -> (o p) c", c=4))
-        base_sb = sb.tile([P, V], F32, name="base_sb")
-        nc.sync.dma_start(out=base_sb[:], in_=base)
 
-        factors = sb.tile([P, 5], F32, name="factors")
-        for j, value in enumerate((256.0, -256.0, -1.0, 512.0, -512.0)):
+        factors = sb.tile([P, 3], F32, name="factors", tag="factors")
+        for j, value in enumerate((256.0, -256.0, -1.0)):
             nc.gpsimd.memset(factors[:, j : j + 1], value)
         warm = sb.tile([P, 1], F32, name="warm")
         nc.scalar.activation(out=warm[:], in_=factors[:, 2:3], func=ACT.Exp)
@@ -72,7 +70,7 @@ def tile_attend_hvrankshares_heads_kernel(tc, hid, voc_words, voc_scales, sw, dh
         def quantise(raw, cast, tag):
             grouped = sb.tile([P, Q, PACK], BF16, name=tag + "_bf", tag=tag + "_bf", align_bytes=64)
             cast(out=grouped[:], in_=raw[:].rearrange("p j q -> p q j"))
-            codes = sb.tile([P, Q], U32, name=tag + "_codes", tag="codes", align_bytes=64)
+            codes = sb.tile([P, Q], U32, name=tag + "_codes", tag=tag + "_codes", align_bytes=64)
             scales = sb.tile([P, Q], U8, name=tag + "_scales", tag=tag + "_scales", align_bytes=64)
             nc.vector.quantize_mx(
                 out=codes[:].bitcast(FP8X4), scales=scales[:], in_=grouped[:].rearrange("p q j -> p (q j)")
@@ -94,14 +92,16 @@ def tile_attend_hvrankshares_heads_kernel(tc, hid, voc_words, voc_scales, sw, dh
             return bank
 
         hq = quantise(hid_raw, nc.vector.tensor_copy, "hid")
+        ident = sb.tile([P, P], F32, name="ident", tag="hid_bf", align_bytes=64)
+        make_identity(nc, ident[:])
         a = sb.tile([P, V], F32, name="a")
         ta = sb.tile([P, V], F32, name="ta")
         maxes = sb.tile([P, CHUNKS], F32, name="maxes")
         dq = None
         for c in range(CHUNKS):
-            bank = score(hq, c, "bank%d" % c)
-            if c == CHUNKS - 1:
+            if c == 2:
                 dq = quantise(dhid_raw, nc.scalar.copy, "dhid")
+            bank = score(hq, c, "bank%d" % c)
             nc.vector.tensor_scalar(
                 out=a[:, cols(c)], in0=bank[:], scalar1=1.0, scalar2=None, op0=ALU.mult, op1=ALU.max,
                 accum_out=maxes[:, c : c + 1],
@@ -109,19 +109,15 @@ def tile_attend_hvrankshares_heads_kernel(tc, hid, voc_words, voc_scales, sw, dh
         ta_banks = [score(dq, c, "bank%d" % (CHUNKS + c)) for c in range(CHUNKS)]
         for c in range(CHUNKS):
             nc.scalar.copy(out=ta[:, cols(c)], in_=ta_banks[c][:])
-        placed1 = sb.tile([P, V], F32, name="placed1", tag="dhid_bf", align_bytes=64)
-        placed2 = sb.tile([P, V], F32, name="placed2", tag="words3", align_bytes=64)
-        nc.gpsimd.memset(placed1[:], 0.0)
-        ident = sb.tile([P, P], F32, name="ident", tag="dhid_scales", align_bytes=64)
-        make_identity(nc, ident[:])
-        nc.gpsimd.memset(placed2[:], 0.0)
+        base_sb = sb.tile([P, V], F32, name="base_sb", tag="words3", align_bytes=64)
+        nc.sync.dma_start(out=base_sb[:], in_=base)
         ax = sb.tile([P, 2, I], F32, name="ax")
         nc.vector.tensor_copy(out=ax[:, 0, :], in_=a[:].indirect(list1[:]))
         neg_max = sb.tile([P, 1], F32, name="neg_max")
         nc.vector.tensor_reduce(out=neg_max[:], in_=maxes[:], axis=AX.X, op=ALU.max, negate=True)
         nc.vector.tensor_copy(out=ax[:, 1, :], in_=a[:].indirect(list2[:]))
 
-        p = sb.tile([P, V], F32, name="p", tag="codes", align_bytes=64)
+        p = sb.tile([P, V], F32, name="p", tag="dhid_codes", align_bytes=64)
         z = sb.tile([P, 1], F32, name="z")
         nc.scalar.activation(out=p[:], in_=a[:], func=ACT.Exp, bias=neg_max[:], accum_out=z[:])
         px = sb.tile([P, 2, I], F32, name="px")
@@ -132,15 +128,27 @@ def tile_attend_hvrankshares_heads_kernel(tc, hid, voc_words, voc_scales, sw, dh
         nc.vector.tensor_copy(out=tx[:, 1, :], in_=ta[:].indirect(list2[:]))
         r = sb.tile([P, 1], F32, name="r")
         nc.vector.reciprocal(out=r[:], in_=z[:])
-        rs = sb.tile([P, 5], F32, name="rs")
+        rs = sb.tile([P, 3], F32, name="rs")
         nc.scalar.activation(out=rs[:], in_=factors[:], func=ACT.Copy, scale=r[:])
         rho, neg_rho, neg_r = rs[:, 0:1], rs[:, 1:2], rs[:, 2:3]
 
-        w_bank = ps.tile([P, 4, P], F32, name="w_bank", tag="bank0")
+        w_bank = ps.tile([P, 4, P], F32, name="w_bank", tag="bank4")
         for c in range(4):
             nc.tensor.transpose(w_bank[:, c, :], w_cols[:, c : c + 1].to_broadcast([P, P]), ident[:])
 
-        sums = [ps.tile([P, BLOCKS, P], F32, name="sum%d" % c, tag="bank%d" % b) for c, b in enumerate((1, 2, 3, 4))]
+        dp = sb.tile([P, I], F32, name="dp", tag="dp")
+        nc.vector.tensor_tensor(out=dp[:], in0=px2, in1=px1, op=ALU.subtract)
+        xp = sb.tile([P, V], F32, name="xp", tag="factors")
+        xz = sb.tile([P, 2], F32, name="xz")
+
+        def make_xp(part, where):
+            nc.vector.scalar_tensor_tensor(
+                out=xp[:, where], in0=ta[:, where], scalar=1.0, in1=p[:, where], op0=ALU.mult, op1=ALU.mult,
+                accum_out=xz[:, part : part + 1],
+            )
+
+        make_xp(0, slice(0, V - BANK))
+        sums = [ps.tile([P, BLOCKS, P], F32, name="sum%d" % c, tag="bank%d" % b) for c, b in enumerate((5, 6, 7, 4))]
 
         def add_turned(c, j, block, start=False, stop=False):
             nc.tensor.matmul(sums[c][:, j, :], block, ident[:], start=start, stop=stop, is_transpose=True)
@@ -149,30 +157,12 @@ def tile_attend_hvrankshares_heads_kernel(tc, hid, voc_words, voc_scales, sw, dh
             for j in range(BLOCKS):
                 add_turned(c, j, base_sb[:, c * BANK + j * P : c * BANK + (j + 1) * P], start=(j == 0))
 
-        xp = [sb.tile([P, BANK], F32, name="xp%d" % c) for c in range(CHUNKS)]
-        xz = sb.tile([P, CHUNKS], F32, name="xz")
-
-        def make_xp(c):
-            nc.vector.scalar_tensor_tensor(
-                out=xp[c][:], in0=ta_banks[c][:], scalar=1.0, in1=p[:, cols(c)], op0=ALU.mult, op1=ALU.mult,
-                accum_out=xz[:, c : c + 1],
-            )
-
-        make_xp(0)
-        dp = sb.tile([P, I], F32, name="dp")
-        nc.vector.tensor_tensor(out=dp[:], in0=px2, in1=px1, op=ALU.subtract)
-        for c in range(1, CHUNKS):
-            make_xp(c)
         th = sb.tile([P, I], F32, name="th")
-        th2 = sb.tile([P, I], F32, name="th2")
+        th2 = sb.tile([P, I], F32, name="th2", tag="th2")
         nc.scalar.activation(out=th[:], in_=dp[:], func=ACT.Tanh, scale=rho)
         nc.scalar.activation(out=th2[:], in_=th[:], func=ACT.Square)
-        tp = sb.tile([P, 2, I], F32, name="tp")
-        for k in range(2):
-            nc.gpsimd.tensor_tensor(out=tp[:, k, :], in0=th[:], in1=px[:, k, :], op=ALU.mult)
-        junk4 = sb.tile([P, 4], F32, name="junk4")
-        neg_mu = sb.tile([P, 1], F32, name="neg_mu")
-        nc.scalar.activation(out=junk4[:], in_=xz[:], func=ACT.Copy, scale=neg_r, accum_out=neg_mu[:])
+        placed1 = sb.tile([P, V], F32, name="placed1", tag="dp")
+        nc.gpsimd.memset(placed1[:], 0.0)
 
         g = sb.tile([P, I], F32, name="g")
         nc.vector.scalar_tensor_tensor(
@@ -183,6 +173,13 @@ def tile_attend_hvrankshares_heads_kernel(tc, hid, voc_words, voc_scales, sw, dh
             op0=ALU.add,
             op1=ALU.mult,
         )
+        make_xp(1, slice(V - BANK, V))
+        placed2 = sb.tile([P, V], F32, name="placed2", tag="th2")
+        nc.gpsimd.memset(placed2[:], 0.0)
+        xz_scaled = sb.tile([P, 2], F32, name="xz_scaled")
+        neg_mu = sb.tile([P, 1], F32, name="neg_mu")
+        nc.scalar.activation(out=xz_scaled[:], in_=xz[:], func=ACT.Copy, scale=neg_r, accum_out=neg_mu[:])
+
         gp = sb.tile([P, 2, I], F32, name="gp")
         b_parts = sb.tile([P, 2], F32, name="b_parts")
         for k, (pxk, factor) in enumerate(((px1, rho), (px2, neg_rho))):
@@ -190,39 +187,46 @@ def tile_attend_hvrankshares_heads_kernel(tc, hid, voc_words, voc_scales, sw, dh
                 out=gp[:, k, :], in0=g[:], scalar=factor, in1=pxk, op0=ALU.mult, op1=ALU.mult,
                 accum_out=b_parts[:, k : k + 1],
             )
-        s_parts = sb.tile([P, 5], F32, name="s_parts")
+        s_parts = sb.tile([P, 7], F32, name="s_parts")
         y = sb.tile([P, 2, I], F32, name="y")
+        whole = slice(0, I)
         halves = [slice(h * I // 2, (h + 1) * I // 2) for h in range(2)]
-        for h, half in enumerate(halves):
+        for n, (k, part) in enumerate(((0, whole), (1, halves[0]), (1, halves[1]))):
             nc.vector.scalar_tensor_tensor(
-                out=y[:, :, half], in0=tx[:, :, half], scalar=neg_mu[:], in1=gp[:, :, half],
-                op0=ALU.add, op1=ALU.mult, accum_out=s_parts[:, h : h + 1],
+                out=y[:, k, part], in0=tx[:, k, part], scalar=neg_mu[:], in1=gp[:, k, part],
+                op0=ALU.add, op1=ALU.mult, accum_out=s_parts[:, n : n + 1],
             )
-        junk2 = sb.tile([P, 2], F32, name="junk2")
-        b_sum = sb.tile([P, 1], F32, name="b_sum")
+        b_scaled = sb.tile([P, 2], F32, name="b_scaled")
+        b_centred = sb.tile([P, 2], F32, name="b_centred")
         beta = sb.tile([P, 1], F32, name="beta")
-        nc.scalar.activation(out=junk2[:], in_=b_parts[:], func=ACT.Copy, accum_out=b_sum[:])
-        nc.scalar.activation(out=beta[:], in_=b_sum[:], func=ACT.Copy, scale=neg_r)
-        nc.scalar.activation(out=s_parts[:, 4:5], in_=b_sum[:], func=ACT.Copy, scale=neg_mu[:])
+        nc.scalar.activation(out=b_scaled[:], in_=b_parts[:], func=ACT.Copy, scale=neg_r, accum_out=beta[:])
+        nc.scalar.activation(
+            out=b_centred[:], in_=b_parts[:], func=ACT.Copy, scale=neg_mu[:], accum_out=s_parts[:, 6:7]
+        )
         for c in range(CHUNKS):
             scaled = sb.tile([P, BANK], F32, name="bxp%d" % c)
-            nc.scalar.activation(out=scaled[:], in_=xp[c][:], func=ACT.Copy, scale=beta[:])
+            nc.scalar.activation(out=scaled[:], in_=xp[:, cols(c)], func=ACT.Copy, scale=beta[:])
             for j in range(BLOCKS):
                 add_turned(c, j, scaled[:, blk(j)])
 
         eg = sb.tile([P, I], F32, name="eg")
+        kk = sb.tile([P, I], F32, name="kk")
         for half in halves:
             nc.vector.tensor_tensor(out=eg[:, half], in0=y[:, 0, half], in1=y[:, 1, half], op=ALU.add)
-        m = sb.tile([P, 2, I], F32, name="m")
-        for k in range(2):
+        for half in halves:
             nc.vector.scalar_tensor_tensor(
-                out=m[:, k, :], in0=tp[:, k, :], scalar=rs[:, 3 + k : 4 + k], in1=eg[:], op0=ALU.mult, op1=ALU.mult,
-                accum_out=s_parts[:, 2 + k : 3 + k],
+                out=kk[:, half], in0=th[:, half], scalar=rho, in1=eg[:, half], op0=ALU.mult, op1=ALU.mult
+            )
+        m = sb.tile([P, 2, I], F32, name="m")
+        for n, (k, part, factor) in enumerate(((0, halves[0], 2.0), (0, halves[1], 2.0), (1, whole, -2.0))):
+            nc.vector.scalar_tensor_tensor(
+                out=m[:, k, part], in0=kk[:, part], scalar=factor, in1=px[:, k, part], op0=ALU.mult, op1=ALU.mult,
+                accum_out=s_parts[:, 3 + n : 4 + n],
             )
         nc.vector.tensor_tensor(out=placed1[:].indirect(list1[:]), in0=y[:, 0, :], in1=m[:, 0, :], op=ALU.add)
         nc.vector.tensor_tensor(out=placed2[:].indirect(list2[:]), in0=y[:, 1, :], in1=m[:, 1, :], op=ALU.add)
 
-        junk5 = sb.tile([P, 5], F32, name="junk5")
+        junk5 = sb.tile([P, 7], F32, name="junk5")
         alpha = sb.tile([P, 1], F32, name="alpha")
         nc.scalar.activation(out=junk5[:], in_=s_parts[:], func=ACT.Copy, scale=neg_r, accum_out=alpha[:])
         p_blocks = p[:].rearrange("p (c j n) -> p c j n", c=CHUNKS, j=BLOCKS)
@@ -237,7 +241,7 @@ def tile_attend_hvrankshares_heads_kernel(tc, hid, voc_words, voc_scales, sw, dh
         for c in range(CHUNKS):
             turned = sb.tile([P, BLOCKS, P], F32, name="turned%d" % c)
             nc.scalar.copy(out=turned[:], in_=sums[c][:])
-            back = ps.tile([P, BLOCKS, P], F32, name="back%d" % c, tag="bank%d" % (5, 6, 7, 0)[c])
+            back = ps.tile([P, BLOCKS, P], F32, name="back%d" % c, tag="bank%d" % c)
             for j in range(BLOCKS):
                 nc.tensor.transpose(back[:, j, :], turned[:, j, :], ident[:])
             pieces = 2 if c in (0, CHUNKS - 1) else 1

from contextlib import ExitStack

import concourse.mybir as mybir
from concourse.masks import make_identity

D, V, Q, I = 512, 2048, 128, 512
FLOPS = 2 * 2 * D * Q * V

F32 = mybir.dt.float32
BF16 = mybir.dt.bfloat16
I32 = mybir.dt.int32
U32 = mybir.dt.uint32
U16 = mybir.dt.uint16
U8 = mybir.dt.uint8
FP8X4 = mybir.dt.float8_e4m3fn_x4
ACT = mybir.ActivationFunctionType
ALU = mybir.AluOpType
AX = mybir.AxisListType

P = 128
PACK = 4
BANK = 512
CHUNKS = V // BANK
BLOCKS = BANK // P


def tile_attend_hvrankshares_heads_kernel(tc, hid, voc_words, voc_scales, sw, dhid, base, offs, offs2, out):
    nc = tc.nc
    with ExitStack() as ctx:
        sb = ctx.enter_context(tc.tile_pool(name="sb", bufs=1))
        ps = ctx.enter_context(tc.psum_pool(name="ps", bufs=1))

        def cols(c):
            return slice(c * BANK, (c + 1) * BANK)

        def blk(j):
            return slice(j * P, (j + 1) * P)

        planes = sb.tile([P, BANK], U8, name="planes", align_bytes=64)
        nc.gpsimd.memset(planes[:].bitcast(I32), 0)
        hid_raw = sb.tile([P, PACK, Q], F32, name="hid_raw")
        dhid_raw = sb.tile([P, PACK, Q], F32, name="dhid_raw")
        words = [sb.tile([P, BANK], U32, name="words%d" % c, tag="words%d" % c, align_bytes=64) for c in range(CHUNKS)]
        voc32 = voc_words[0].rearrange("p n t -> p (n t)").bitcast(I32)
        scales32 = voc_scales[0].bitcast(I32)

        nc.sync.dma_start(out=hid_raw[:], in_=hid.rearrange("(p j) q -> p j q", j=PACK))
        for quad in range(4):
            nc.sync.dma_start(
                out=planes[32 * quad : 32 * quad + 16, :].bitcast(I32),
                in_=scales32[4 * quad : 4 * quad + 4, :].rearrange("r (c n) -> c r n", c=CHUNKS),
            )
        for c in range(CHUNKS):
            if c == 2:
                nc.sync.dma_start(out=dhid_raw[:], in_=dhid.rearrange("(p j) q -> p j q", j=PACK))
            nc.sync.dma_start(out=words[c][:].bitcast(I32), in_=voc32[:, cols(c)])
        list1 = sb.tile([P, I // 16], U16, name="list1")
        list2 = sb.tile([P, I // 16], U16, name="list2")
        nc.sync.dma_start(list1[:], offs)
        nc.sync.dma_start(list2[:], offs2)
        w_cols = sb.tile([P, 4], F32, name="w_cols")
        nc.sync.dma_start(out=w_cols[:], in_=sw.rearrange("o (p c) -> (o p) c", c=4))

        factors = sb.tile([P, 3], F32, name="factors", tag="factors")
        for j, value in enumerate((256.0, -256.0, -1.0)):
            nc.gpsimd.memset(factors[:, j : j + 1], value)
        warm = sb.tile([P, 1], F32, name="warm")
        nc.scalar.activation(out=warm[:], in_=factors[:, 2:3], func=ACT.Exp)

        def quantise(raw, cast, tag):
            grouped = sb.tile([P, Q, PACK], BF16, name=tag + "_bf", tag=tag + "_bf", align_bytes=64)
            cast(out=grouped[:], in_=raw[:].rearrange("p j q -> p q j"))
            codes = sb.tile([P, Q], U32, name=tag + "_codes", tag=tag + "_codes", align_bytes=64)
            scales = sb.tile([P, Q], U8, name=tag + "_scales", tag=tag + "_scales", align_bytes=64)
            nc.vector.quantize_mx(
                out=codes[:].bitcast(FP8X4), scales=scales[:], in_=grouped[:].rearrange("p q j -> p (q j)")
            )
            return codes, scales

        def score(operand, c, tag):
            codes, scales = operand
            bank = ps.tile([P, BANK], F32, name=tag, tag=tag)
            nc.tensor.matmul_mx(
                out=bank[:],
                lhsT=codes[:].bitcast(FP8X4),
                lhsT_scale=scales[:],
                rhs=words[c][:].bitcast(FP8X4),
                rhs_scale=planes[4 * c : P, :],
                start=True,
                stop=True,
            )
            return bank

        hq = quantise(hid_raw, nc.vector.tensor_copy, "hid")
        ident = sb.tile([P, P], F32, name="ident", tag="hid_bf", align_bytes=64)
        make_identity(nc, ident[:])
        a = sb.tile([P, V], F32, name="a")
        ta = sb.tile([P, V], F32, name="ta")
        maxes = sb.tile([P, CHUNKS], F32, name="maxes")
        dq = None
        for c in range(CHUNKS):
            if c == 2:
                dq = quantise(dhid_raw, nc.scalar.copy, "dhid")
            bank = score(hq, c, "bank%d" % c)
            nc.vector.tensor_scalar(
                out=a[:, cols(c)], in0=bank[:], scalar1=1.0, scalar2=None, op0=ALU.mult, op1=ALU.max,
                accum_out=maxes[:, c : c + 1],
            )
        ta_banks = [score(dq, c, "bank%d" % (CHUNKS + c)) for c in range(CHUNKS)]
        for c in range(CHUNKS):
            nc.scalar.copy(out=ta[:, cols(c)], in_=ta_banks[c][:])
        base_sb = sb.tile([P, V], F32, name="base_sb", tag="words3", align_bytes=64)
        nc.sync.dma_start(out=base_sb[:], in_=base)
        ax = sb.tile([P, 2, I], F32, name="ax")
        nc.vector.tensor_copy(out=ax[:, 0, :], in_=a[:].indirect(list1[:]))
        neg_max = sb.tile([P, 1], F32, name="neg_max")
        nc.vector.tensor_reduce(out=neg_max[:], in_=maxes[:], axis=AX.X, op=ALU.max, negate=True)
        nc.vector.tensor_copy(out=ax[:, 1, :], in_=a[:].indirect(list2[:]))

        p = sb.tile([P, V], F32, name="p", tag="dhid_codes", align_bytes=64)
        z = sb.tile([P, 1], F32, name="z")
        nc.scalar.activation(out=p[:], in_=a[:], func=ACT.Exp, bias=neg_max[:], accum_out=z[:])
        px = sb.tile([P, 2, I], F32, name="px")
        nc.scalar.activation(out=px[:], in_=ax[:], func=ACT.Exp, bias=neg_max[:])
        px1, px2 = px[:, 0, :], px[:, 1, :]
        tx = sb.tile([P, 2, I], F32, name="tx")
        nc.vector.tensor_copy(out=tx[:, 0, :], in_=ta[:].indirect(list1[:]))
        nc.vector.tensor_copy(out=tx[:, 1, :], in_=ta[:].indirect(list2[:]))
        r = sb.tile([P, 1], F32, name="r")
        nc.vector.reciprocal(out=r[:], in_=z[:])
        rs = sb.tile([P, 3], F32, name="rs")
        nc.scalar.activation(out=rs[:], in_=factors[:], func=ACT.Copy, scale=r[:])
        rho, neg_rho, neg_r = rs[:, 0:1], rs[:, 1:2], rs[:, 2:3]

        w_bank = ps.tile([P, 4, P], F32, name="w_bank", tag="bank4")
        for c in range(4):
            nc.tensor.transpose(w_bank[:, c, :], w_cols[:, c : c + 1].to_broadcast([P, P]), ident[:])

        dp = sb.tile([P, I], F32, name="dp", tag="dp")
        nc.vector.tensor_tensor(out=dp[:], in0=px2, in1=px1, op=ALU.subtract)
        xp = sb.tile([P, V], F32, name="xp", tag="factors")
        xz = sb.tile([P, 2], F32, name="xz")

        def make_xp(part, where):
            nc.vector.scalar_tensor_tensor(
                out=xp[:, where], in0=ta[:, where], scalar=1.0, in1=p[:, where], op0=ALU.mult, op1=ALU.mult,
                accum_out=xz[:, part : part + 1],
            )

        make_xp(0, slice(0, V - BANK))
        sums = [ps.tile([P, BLOCKS, P], F32, name="sum%d" % c, tag="bank%d" % b) for c, b in enumerate((5, 6, 7, 4))]

        def add_turned(c, j, block, start=False, stop=False):
            nc.tensor.matmul(sums[c][:, j, :], block, ident[:], start=start, stop=stop, is_transpose=True)

        for c in range(CHUNKS):
            for j in range(BLOCKS):
                add_turned(c, j, base_sb[:, c * BANK + j * P : c * BANK + (j + 1) * P], start=(j == 0))

        th = sb.tile([P, I], F32, name="th")
        th2 = sb.tile([P, I], F32, name="th2", tag="th2")
        nc.scalar.activation(out=th[:], in_=dp[:], func=ACT.Tanh, scale=rho)
        nc.scalar.activation(out=th2[:], in_=th[:], func=ACT.Square)
        placed1 = sb.tile([P, V], F32, name="placed1", tag="dp")
        nc.gpsimd.memset(placed1[:], 0.0)

        g = sb.tile([P, I], F32, name="g")
        nc.vector.scalar_tensor_tensor(
            out=g[:].rearrange("p (n c) -> p n c", c=4),
            in0=th2[:].rearrange("p (n c) -> p n c", c=4),
            scalar=-1.0,
            in1=w_bank[:].rearrange("p c n -> p n c"),
            op0=ALU.add,
            op1=ALU.mult,
        )
        make_xp(1, slice(V - BANK, V))
        placed2 = sb.tile([P, V], F32, name="placed2", tag="th2")
        nc.gpsimd.memset(placed2[:], 0.0)
        xz_scaled = sb.tile([P, 2], F32, name="xz_scaled")
        neg_mu = sb.tile([P, 1], F32, name="neg_mu")
        nc.scalar.activation(out=xz_scaled[:], in_=xz[:], func=ACT.Copy, scale=neg_r, accum_out=neg_mu[:])

        gp = sb.tile([P, 2, I], F32, name="gp")
        b_parts = sb.tile([P, 2], F32, name="b_parts")
        for k, (pxk, factor) in enumerate(((px1, rho), (px2, neg_rho))):
            nc.vector.scalar_tensor_tensor(
                out=gp[:, k, :], in0=g[:], scalar=factor, in1=pxk, op0=ALU.mult, op1=ALU.mult,
                accum_out=b_parts[:, k : k + 1],
            )
        s_parts = sb.tile([P, 7], F32, name="s_parts")
        y = sb.tile([P, 2, I], F32, name="y")
        whole = slice(0, I)
        halves = [slice(h * I // 2, (h + 1) * I // 2) for h in range(2)]
        for n, (k, part) in enumerate(((0, whole), (1, halves[0]), (1, halves[1]))):
            nc.vector.scalar_tensor_tensor(
                out=y[:, k, part], in0=tx[:, k, part], scalar=neg_mu[:], in1=gp[:, k, part],
                op0=ALU.add, op1=ALU.mult, accum_out=s_parts[:, n : n + 1],
            )
        b_scaled = sb.tile([P, 2], F32, name="b_scaled")
        b_centred = sb.tile([P, 2], F32, name="b_centred")
        beta = sb.tile([P, 1], F32, name="beta")
        nc.scalar.activation(out=b_scaled[:], in_=b_parts[:], func=ACT.Copy, scale=neg_r, accum_out=beta[:])
        nc.scalar.activation(
            out=b_centred[:], in_=b_parts[:], func=ACT.Copy, scale=neg_mu[:], accum_out=s_parts[:, 6:7]
        )
        for c in range(CHUNKS):
            scaled = sb.tile([P, BANK], F32, name="bxp%d" % c)
            nc.scalar.activation(out=scaled[:], in_=xp[:, cols(c)], func=ACT.Copy, scale=beta[:])
            for j in range(BLOCKS):
                add_turned(c, j, scaled[:, blk(j)])

        eg = sb.tile([P, I], F32, name="eg")
        kk = sb.tile([P, I], F32, name="kk")
        for half in halves:
            nc.vector.tensor_tensor(out=eg[:, half], in0=y[:, 0, half], in1=y[:, 1, half], op=ALU.add)
        for half in halves:
            nc.vector.scalar_tensor_tensor(
                out=kk[:, half], in0=th[:, half], scalar=rho, in1=eg[:, half], op0=ALU.mult, op1=ALU.mult
            )
        m = sb.tile([P, 2, I], F32, name="m")
        for n, (k, part, factor) in enumerate(((0, halves[0], 2.0), (0, halves[1], 2.0), (1, whole, -2.0))):
            nc.vector.scalar_tensor_tensor(
                out=m[:, k, part], in0=kk[:, part], scalar=factor, in1=px[:, k, part], op0=ALU.mult, op1=ALU.mult,
                accum_out=s_parts[:, 3 + n : 4 + n],
            )
        nc.vector.tensor_tensor(out=placed1[:].indirect(list1[:]), in0=y[:, 0, :], in1=m[:, 0, :], op=ALU.add)
        nc.vector.tensor_tensor(out=placed2[:].indirect(list2[:]), in0=y[:, 1, :], in1=m[:, 1, :], op=ALU.add)

        junk5 = sb.tile([P, 7], F32, name="junk5")
        alpha = sb.tile([P, 1], F32, name="alpha")
        nc.scalar.activation(out=junk5[:], in_=s_parts[:], func=ACT.Copy, scale=neg_r, accum_out=alpha[:])
        p_blocks = p[:].rearrange("p (c j n) -> p c j n", c=CHUNKS, j=BLOCKS)
        for j in range(BLOCKS):
            scaled = sb.tile([P, CHUNKS, P], F32, name="ap%d" % j)
            nc.scalar.activation(out=scaled[:], in_=p_blocks[:, :, j, :], func=ACT.Copy, scale=alpha[:])
            for c in range(CHUNKS):
                add_turned(c, j, scaled[:, c, :])
        for c in range(CHUNKS):
            for j in range(BLOCKS):
                add_turned(c, j, placed1[:, c * BANK + j * P : c * BANK + (j + 1) * P], stop=(j == BLOCKS - 1))
        for c in range(CHUNKS):
            turned = sb.tile([P, BLOCKS, P], F32, name="turned%d" % c)
            nc.scalar.copy(out=turned[:], in_=sums[c][:])
            back = ps.tile([P, BLOCKS, P], F32, name="back%d" % c, tag="bank%d" % c)
            for j in range(BLOCKS):
                nc.tensor.transpose(back[:, j, :], turned[:, j, :], ident[:])
            pieces = 2 if c in (0, CHUNKS - 1) else 1
            width = BANK // pieces
            for h in range(pieces):
                result = sb.tile([P, width], F32, name="result%d_%d" % (c, h))
                where = slice(c * BANK + h * width, c * BANK + (h + 1) * width)
                nc.vector.tensor_tensor(
                    out=result[:],
                    in0=back[:].rearrange("p j n -> p (j n)")[:, h * width : (h + 1) * width],
                    in1=placed2[:, where],
                    op=ALU.add,
                )
                nc.sync.dma_start(out=out[:, where], in_=result[:])
